import numpy as np
import ml_dtypes


def mxq(x, axis, fmt="e4m3"):
    dtype, down = {"e4m3": (ml_dtypes.float8_e4m3fn, 7), "e5m2": (ml_dtypes.float8_e5m2, 14)}[fmt]
    v = np.moveaxis(np.asarray(x, np.float32).astype(ml_dtypes.bfloat16).astype(np.float64), axis, -1)
    blocks = v.reshape(v.shape[:-1] + (-1, 32))
    amax = np.abs(blocks).max(-1, keepdims=True)
    byte = np.maximum(np.where(amax > 0, np.frexp(amax)[1] - 1 + 127, 0) - down, 1)
    scale = np.exp2(byte - 127.0)
    codes = (blocks / scale).astype(np.float32).astype(dtype).astype(np.float64)
    return np.moveaxis((codes * scale).reshape(v.shape), -1, axis)


WIDE = False


def mx_kscale(k):
    if not WIDE:
        return np.ones(k)
    levels = np.array([10, -10, 5, -5, 0])
    if k % 512:
        return np.exp2(np.random.permutation(np.resize(levels, k // 32))).repeat(32)
    a = np.empty((k // 512, 16))
    for p in range(k // 512):
        a[p, :8] = np.random.permutation(np.resize(levels, 8))
        for g in range(8):
            far = levels[np.abs(levels - a[p, g]) >= 10]
            a[p, g + 8] = far[np.random.randint(len(far))]
    return np.exp2(a.ravel()).repeat(32)


def f64(x):
    return np.asarray(x).astype(np.float64)


def striped(idx):
    return np.tile(idx.reshape(-1, 16).T, (8, 1)).astype(np.uint16)


def unstriped(offs):
    return offs[:16].T.reshape(-1).astype(np.int64)


def striped8(idx):
    return np.concatenate([x.reshape(-1, 16).T for x in idx]).astype(np.uint16)


def runs(offs, k):
    lists = np.stack([offs[16 * r : 16 * r + 16].T.reshape(-1) for r in range(8)]).astype(np.int64)
    return lists[np.arange(k) % 512 // 64]


def pack_weight(w):
    k, n = w.shape
    w = f64(np.asarray(w, np.float32).astype(ml_dtypes.bfloat16)).reshape(k // 32, 32, n)
    amax = np.abs(w).max(1)
    byte = np.clip(np.where(amax > 0, np.frexp(amax)[1] - 1 + 127 - 7, 1), 1, 254)
    scaled = (w * np.exp2(127.0 - byte)[:, None, :]).reshape(k, n).astype(np.float32)
    words = np.ascontiguousarray(scaled.reshape(k // 512, 128, 4, n).transpose(0, 1, 3, 2)).astype(ml_dtypes.float8_e4m3fn).view(np.uint8)
    return words, np.ascontiguousarray(byte.astype(np.uint8).reshape(k // 512, 16, n))


def unpack_weight(words, scales):
    g, p, n, _ = words.shape
    vals = np.ascontiguousarray(words).view(ml_dtypes.float8_e4m3fn).astype(np.float64) * np.repeat(np.exp2(scales.astype(np.float64) - 127.0), 8, axis=1)[..., None]
    return vals.transpose(0, 1, 3, 2).reshape(g * 512, n)


K, T, S, N, G, H = 512, 1024, 256, 512, 2048, 512


def setup_inputs():
    n = np.random.standard_normal
    s = mx_kscale(K)[:, None]
    u = mx_kscale(K)
    packed_xT = pack_weight(n((K, T)) * s)
    packed_dT = pack_weight(n((K, G)) / s)
    return {
        "x_words": packed_xT[0],
        "x_scales": packed_xT[1],
        "d_words": packed_dT[0],
        "d_scales": packed_dT[1],
        "gn": (np.random.uniform(0.5, 1.5, (H, 1)) * u[:, None]).astype(np.float32),
        "w1": (n((H, N)) / np.sqrt(H) / u[:, None]).astype(np.float32),
        "offs": striped(np.random.permutation(T)[:S]),
        "k1": striped8(np.random.randint(0, G, (8, H))),
        "two": striped(np.random.permutation(T)[:S]),
        "k2": striped8(np.random.randint(0, G, (8, H))),
        "n1": striped(np.random.permutation(S)),
        "n2": striped(np.random.permutation(S)),
        "n3": striped8(np.stack([np.random.permutation(S) for _ in range(8)])),
        "n4": striped8(np.stack([np.random.permutation(S) for _ in range(8)])),
        "n5": striped8(np.stack([np.random.permutation(S) for _ in range(8)])),
    }


def reference(x_words, x_scales, d_words, d_scales, gn, w1, offs, k1, two, k2, n1, n2, n3, n4, n5):
    d_k1 = unpack_weight(d_words, d_scales)[np.arange(K)[:, None], runs(k1, K)]
    xq = unpack_weight(x_words, x_scales)[:, unstriped(offs)]
    a = 0.0625 * (d_k1.T @ xq)
    d_k2 = unpack_weight(d_words, d_scales)[np.arange(K)[:, None], runs(k2, K)]
    x_two = unpack_weight(x_words, x_scales)[:, unstriped(two)]
    b = 0.0625 * (d_k2.T @ x_two)
    z = f64(gn) * (a[:, unstriped(n1)] - (np.tanh(b) * b[:, unstriped(n2)]))
    h = mxq(f64(w1), 0, "e4m3").T @ mxq(z, 0, "e4m3")
    return 0.75 * (h * (h[np.arange(N)[:, None], runs(n3, N)]) + (h[np.arange(N)[:, None], runs(n4, N)]) * (h[np.arange(N)[:, None], runs(n5, N)]))

@@ -1,0 +1,188 @@
+from contextlib import ExitStack
+
+import concourse.mybir as mybir
+
+K, T, S, N, G, H = 512, 1024, 256, 512, 2048, 512
+FLOPS = 2 * K * H * S * 2 + 2 * H * N * S
+
+F32 = mybir.dt.float32
+BF16 = mybir.dt.bfloat16
+I32 = mybir.dt.int32
+U32 = mybir.dt.uint32
+U16 = mybir.dt.uint16
+U8 = mybir.dt.uint8
+FP8X4 = mybir.dt.float8_e4m3fn_x4
+ALU = mybir.AluOpType
+ACT = mybir.ActivationFunctionType
+
+P = 128
+PLANES = 4
+HALF = S // 2
+SCALAR_N2_PLANES = 2
+
+
+def tile_picked_twpqsoftbdot_none_p_kernel(tc, x_words, x_scales, d_words, d_scales, gn, w1, offs, k1, two, k2, n1, n2, n3, n4, n5, out):
+    nc = tc.nc
+    with ExitStack() as ctx:
+        lists = ctx.enter_context(tc.tile_pool(name="lists", bufs=1))
+        sb = ctx.enter_context(tc.tile_pool(name="sb", bufs=1))
+        reused = ctx.enter_context(tc.tile_pool(name="reused", bufs=1))
+        psum = ctx.enter_context(tc.psum_pool(name="psum", bufs=1))
+
+        def load_list(src, name):
+            tile = lists.tile(list(src.shape), U16, name=name)
+            nc.sync.dma_start(tile[:], src)
+            return tile
+
+        def half_of(offsets, half):
+            return offsets[:, half * (HALF // 16) : (half + 1) * (HALF // 16)]
+
+        d_scale_table = sb.tile([P, G], U8, name="d_scale_table", align_bytes=64)
+        k2_list = load_list(k2, "k2_list")
+        k1_list = load_list(k1, "k1_list")
+        d_scale_rows = d_scales[0].bitcast(I32).rearrange("(run r) w -> r run w", r=2)
+        for r in range(2):
+            nc.sync.dma_start(d_scale_table[r:P:2, :].bitcast(I32), d_scale_rows[r].unsqueeze(1).to_broadcast([8, 8, G // 4]))
+
+        two_list = load_list(two, "two_list")
+        offs_list = load_list(offs, "offs_list")
+        w_raw = sb.tile([P, PLANES, N], F32, name="w_raw", align_bytes=64)
+        nc.sync.dma_start(w_raw[:], w1.rearrange("(p j) m -> p j m", j=PLANES))
+        d_word_table = sb.tile([P, G], U32, name="d_word_table", align_bytes=64)
+        nc.sync.dma_start(d_word_table[:].bitcast(I32), d_words[0].rearrange("p n t -> p (n t)").bitcast(I32))
+        x_word_table = reused.tile([P, T], U32, name="x_word_table", align_bytes=64, offset=T)
+        nc.sync.dma_start(x_word_table[:].bitcast(I32), x_words[0].rearrange("p n t -> p (n t)").bitcast(I32))
+
+        x_scale_table = reused.tile([P, T], U8, name="x_scale_table", align_bytes=64, offset=0)
+        for q in range(4):
+            rows = x_scales[0].bitcast(I32)[4 * q : 4 * q + 4, :]
+            nc.gpsimd.dma_start(x_scale_table[32 * q : 32 * q + 32, :].bitcast(I32), rows.unsqueeze(0).to_broadcast([8, 4, T // 4]))
+        gain = sb.tile([P, PLANES], F32, name="gain")
+        nc.gpsimd.dma_start(gain[:], gn.rearrange("(p t) o -> p (t o)", t=PLANES))
+        gain16 = sb.tile([P, PLANES], F32, name="gain16")
+        nc.gpsimd.tensor_scalar(gain16[:], gain[:], 0.0625, 0.0, ALU.mult, ALU.add)
+
+        h_rows = [sb.tile([P, 2 * S], F32, name=f"h_rows{t}", align_bytes=64) for t in range(PLANES)]
+        for t in range(PLANES):
+            nc.vector.memset(h_rows[t][:, S:], 0.0)
+
+        n2_list = load_list(n2, "n2_list")
+        n1_list = load_list(n1, "n1_list")
+        n3_list = load_list(n3, "n3_list")
+        n4_list = load_list(n4, "n4_list")
+        n5_list = load_list(n5, "n5_list")
+
+        w_bf = sb.tile([P, PLANES * N], BF16, name="w_bf", align_bytes=64)
+        nc.scalar.copy(
+            w_bf[:].rearrange("p (t m j) -> p m j t", t=PLANES, j=PLANES),
+            w_raw[:].rearrange("p j (m t) -> p m j t", t=PLANES),
+        )
+
+        d_scale_picked = sb.tile([P, 2 * H], U8, name="d_scale_picked", align_bytes=64)
+        nc.vector.tensor_copy(d_scale_picked[:, :H], d_scale_table[:].indirect(k2_list[:]))
+        nc.vector.tensor_copy(d_scale_picked[:, H:], d_scale_table[:].indirect(k1_list[:]))
+        d_scale_dealt = sb.tile([P, 2 * H], U8, name="d_scale_dealt", align_bytes=64)
+        nc.vector.tensor_copy(
+            d_scale_dealt[:].rearrange("p (t mm i) -> p mm t i", t=PLANES, i=16),
+            d_scale_picked[:].rearrange("p (mm i t) -> p mm t i", t=PLANES, i=16),
+        )
+        for r in range(2):
+            nc.sync.dma_start(d_scale_dealt[2 + r : P : 32, :].bitcast(I32), d_scale_dealt[16 + r : P : 32, :].bitcast(I32))
+
+        def coded_product(which, k_list, x_list, name, d_picked):
+            x_picked = sb.tile([P, S], U32, name=f"x_picked_{name}", align_bytes=64)
+            nc.vector.tensor_copy(x_picked[:], x_word_table[:].indirect(x_list[:]))
+            x_scale_picked = sb.tile([P, S], U8, name=f"x_scale_picked_{name}", align_bytes=64)
+            nc.vector.tensor_copy(x_scale_picked[:], x_scale_table[:].indirect(x_list[:]))
+            nc.vector.tensor_copy(d_picked[:], d_word_table[:].indirect(k_list[:]))
+            d_dealt = sb.tile([P, H], U32, name=f"d_dealt_{name}", align_bytes=64)
+            nc.vector.tensor_copy(
+                d_dealt[:].rearrange("p (t mm i) -> p mm t i", t=PLANES, i=4),
+                d_picked[:].rearrange("p (mm i t) -> p mm t i", t=PLANES, i=4),
+            )
+            banks = []
+            for t in range(PLANES):
+                bank = psum.tile([P, S], F32, name=f"bank_{name}{t}", tag=f"bank_{name}{t}")
+                first = (2 * t + which) * P
+                nc.tensor.matmul_mx(
+                    out=bank[:],
+                    lhsT=d_dealt[:, t * P : (t + 1) * P].bitcast(FP8X4),
+                    lhsT_scale=d_scale_dealt[:, first : first + P],
+                    rhs=x_picked[:].bitcast(FP8X4),
+                    rhs_scale=x_scale_picked[:],
+                    start=True,
+                    stop=True,
+                )
+                banks.append(bank)
+            return banks
+
+        b_banks = coded_product(0, k2_list, two_list, "b", sb.tile([P, H], U32, name="d_picked_b", align_bytes=64))
+        tanh_b = sb.tile([P, PLANES, S], F32, name="tanh_b", align_bytes=64)
+        b_rows = [sb.tile([P, S], F32, name=f"b_rows{t}", align_bytes=64) for t in range(PLANES)]
+        for t in range(PLANES):
+            nc.scalar.activation(tanh_b[:, t, :], b_banks[t][:], ACT.Tanh, scale=0.0625)
+            nc.scalar.activation(b_rows[t][:], b_banks[t][:], ACT.Copy, scale=gain16[:, t : t + 1])
+        b_picked = sb.tile([P, SCALAR_N2_PLANES, S], F32, name="b_picked", align_bytes=64)
+        for t in range(SCALAR_N2_PLANES):
+            for half in range(2):
+                cols = slice(half * HALF, (half + 1) * HALF)
+                nc.scalar.activation(b_picked[:, t, cols], b_rows[t][:].indirect(half_of(n2_list, half)), ACT.Copy)
+
+        a_banks = coded_product(1, k1_list, offs_list, "a", reused.tile([P, H], U32, name="d_picked_a", align_bytes=64, offset=0))
+
+        w_codes = reused.tile([P, N], U32, name="w_codes", align_bytes=64, offset=0)
+        w_scales = sb.tile([P, N], U8, name="w_scales", align_bytes=64)
+        nc.vector.quantize_mx(out=w_codes[:].bitcast(FP8X4), scales=w_scales[:], in_=w_bf[:])
+
+        a_rows = [sb.tile([P, S], F32, name=f"a_rows{t}", align_bytes=64) for t in range(PLANES)]
+        for t in range(PLANES):
+            nc.vector.tensor_scalar(a_rows[t][:], a_banks[t][:], gain16[:, t : t + 1], None, ALU.mult)
+
+        gated = sb.tile([P, PLANES, S], F32, name="gated", align_bytes=64)
+        nc.vector.tensor_tensor(gated[:, :SCALAR_N2_PLANES, :], b_picked[:], tanh_b[:, :SCALAR_N2_PLANES, :], ALU.mult)
+
+        a_picked = sb.tile([P, PLANES, S], F32, name="a_picked", align_bytes=64)
+        h_banks = [psum.tile([P, S], F32, name=f"bank_h{t}", tag=f"bank_b{t}") for t in range(PLANES)]
+        for half in range(2):
+            cols = slice(half * HALF, (half + 1) * HALF)
+            for t in range(PLANES):
+                nc.scalar.activation(a_picked[:, t, cols], a_rows[t][:].indirect(half_of(n1_list, half)), ACT.Copy)
+            for t in range(SCALAR_N2_PLANES, PLANES):
+                nc.vector.tensor_tensor(gated[:, t, cols], b_rows[t][:].indirect(half_of(n2_list, half)), tanh_b[:, t, cols], ALU.mult)
+            z_bf = sb.tile([P, HALF * PLANES], BF16, name=f"z_bf{half}", align_bytes=64)
+            nc.vector.tensor_tensor(
+                z_bf[:].rearrange("p (c i t) -> p c t i", t=PLANES, i=4),
+                a_picked[:, :, cols].rearrange("p t (c i) -> p c t i", i=4),
+                gated[:, :, cols].rearrange("p t (c i) -> p c t i", i=4),
+                ALU.subtract,
+            )
+            z_codes = sb.tile([P, HALF], U32, name=f"z_codes{half}", align_bytes=64)
+            z_scales = sb.tile([P, HALF], U8, name=f"z_scales{half}", align_bytes=64)
+            nc.vector.quantize_mx(out=z_codes[:].bitcast(FP8X4), scales=z_scales[:], in_=z_bf[:])
+            for t in range(PLANES):
+                nc.tensor.matmul_mx(
+                    out=h_banks[t][:, cols],
+                    lhsT=w_codes[:, t * P : (t + 1) * P].bitcast(FP8X4),
+                    lhsT_scale=w_scales[:, t * P : (t + 1) * P],
+                    rhs=z_codes[:].bitcast(FP8X4),
+                    rhs_scale=z_scales[:],
+                    start=True,
+                    stop=True,
+                )
+
+        out_rows = out.rearrange("(p t) c -> t p c", t=PLANES)
+        for t in range(PLANES):
+            nc.vector.tensor_copy(h_rows[t][:, :S], h_banks[t][:])
+        for t in range(PLANES):
+            picked = []
+            for name, offsets in (("n3", n3_list), ("n4", n4_list), ("n5", n5_list)):
+                tile = sb.tile([P, S], F32, name=f"h_{name}_{t}", align_bytes=64)
+                nc.scalar.activation(tile[:], h_rows[t][:].indirect(offsets[:]), ACT.Copy)
+                picked.append(tile)
+            first = sb.tile([P, S], F32, name=f"first{t}", align_bytes=64)
+            nc.vector.scalar_tensor_tensor(first[:], picked[0][:], 0.75, h_rows[t][:, :S], ALU.mult, ALU.mult)
+            second = sb.tile([P, S], F32, name=f"second{t}", align_bytes=64)
+            nc.vector.scalar_tensor_tensor(second[:], picked[1][:], 0.75, picked[2][:], ALU.mult, ALU.mult)
+            result = sb.tile([P, S], F32, name=f"result{t}", align_bytes=64)
+            nc.vector.tensor_tensor(result[:], first[:], second[:], ALU.add)
+            nc.sync.dma_start(out_rows[t], result[:])

@@ -1,6 +1,7 @@
 from contextlib import ExitStack
 
 import concourse.mybir as mybir
+from concourse.masks import make_identity
 
 K, T, S, N, G, H = 512, 1024, 256, 512, 2048, 512
 FLOPS = 2 * K * H * S * 2 + 2 * H * N * S
@@ -18,7 +19,8 @@ ACT = mybir.ActivationFunctionType
 P = 128
 PLANES = 4
 HALF = S // 2
-SCALAR_N2_PLANES = 2
+SPARE = 16
+VECTOR_A_COPIES = 2
 
 
 def tile_picked_twpqsoftbdot_none_p_kernel(tc, x_words, x_scales, d_words, d_scales, gn, w1, offs, k1, two, k2, n1, n2, n3, n4, n5, out):
@@ -34,43 +36,42 @@ def tile_picked_twpqsoftbdot_none_p_kernel(tc, x_words, x_scales, d_words, d_sca
             nc.sync.dma_start(tile[:], src)
             return tile
 
-        def half_of(offsets, half):
-            return offsets[:, half * (HALF // 16) : (half + 1) * (HALF // 16)]
-
-        d_scale_table = sb.tile([P, G], U8, name="d_scale_table", align_bytes=64)
         k2_list = load_list(k2, "k2_list")
+        d_scale_table = sb.tile([P, G], U8, name="d_scale_table", align_bytes=64)
+        nc.sync.dma_start(d_scale_table[:].bitcast(I32), d_scales[0].bitcast(I32).unsqueeze(1).to_broadcast([16, 8, G // 4]))
         k1_list = load_list(k1, "k1_list")
-        d_scale_rows = d_scales[0].bitcast(I32).rearrange("(run r) w -> r run w", r=2)
-        for r in range(2):
-            nc.sync.dma_start(d_scale_table[r:P:2, :].bitcast(I32), d_scale_rows[r].unsqueeze(1).to_broadcast([8, 8, G // 4]))
-
-        two_list = load_list(two, "two_list")
-        offs_list = load_list(offs, "offs_list")
-        w_raw = sb.tile([P, PLANES, N], F32, name="w_raw", align_bytes=64)
-        nc.sync.dma_start(w_raw[:], w1.rearrange("(p j) m -> p j m", j=PLANES))
         d_word_table = sb.tile([P, G], U32, name="d_word_table", align_bytes=64)
         nc.sync.dma_start(d_word_table[:].bitcast(I32), d_words[0].rearrange("p n t -> p (n t)").bitcast(I32))
+        w_raw = sb.tile([P, PLANES, N], F32, name="w_raw", align_bytes=64)
+        for j in range(PLANES):
+            nc.sync.dma_start(w_raw[:, j, :], w1.rearrange("(q j e) m -> j q e m", j=PLANES, e=8)[j])
         x_word_table = reused.tile([P, T], U32, name="x_word_table", align_bytes=64, offset=T)
         nc.sync.dma_start(x_word_table[:].bitcast(I32), x_words[0].rearrange("p n t -> p (n t)").bitcast(I32))
+        two_list = load_list(two, "two_list")
+        offs_list = load_list(offs, "offs_list")
 
+        gain_rows = sb.tile([P, P], F32, name="gain_rows", align_bytes=64)
+        nc.gpsimd.memset(gain_rows[:], 0.0)
+        nc.gpsimd.dma_start(gain_rows[:PLANES, :].rearrange("t (q e) -> t q e", e=8), gn.rearrange("(q t e) o -> t q (e o)", t=PLANES, e=8))
         x_scale_table = reused.tile([P, T], U8, name="x_scale_table", align_bytes=64, offset=0)
         for q in range(4):
             rows = x_scales[0].bitcast(I32)[4 * q : 4 * q + 4, :]
             nc.gpsimd.dma_start(x_scale_table[32 * q : 32 * q + 32, :].bitcast(I32), rows.unsqueeze(0).to_broadcast([8, 4, T // 4]))
-        gain = sb.tile([P, PLANES], F32, name="gain")
-        nc.gpsimd.dma_start(gain[:], gn.rearrange("(p t) o -> p (t o)", t=PLANES))
+        identity = sb.tile([P, P], F32, name="identity", align_bytes=64)
+        make_identity(nc, identity[:])
+        gain_bank = psum.tile([P, P], F32, name="gain_bank", tag="bank_a3")
+        nc.tensor.transpose(gain_bank[:], gain_rows[:], identity[:])
         gain16 = sb.tile([P, PLANES], F32, name="gain16")
-        nc.gpsimd.tensor_scalar(gain16[:], gain[:], 0.0625, 0.0, ALU.mult, ALU.add)
+        nc.scalar.activation(gain16[:], gain_bank[:, :PLANES], ACT.Copy, scale=0.0625)
 
+        a_rows = [sb.tile([P, S + SPARE], F32, name=f"a_rows{t}", align_bytes=64) for t in range(PLANES)]
+        b_rows = [sb.tile([P, S + SPARE], F32, name=f"b_rows{t}", align_bytes=64) for t in range(PLANES)]
         h_rows = [sb.tile([P, 2 * S], F32, name=f"h_rows{t}", align_bytes=64) for t in range(PLANES)]
-        for t in range(PLANES):
-            nc.vector.memset(h_rows[t][:, S:], 0.0)
+        for window in a_rows + b_rows + h_rows:
+            nc.vector.memset(window[:, S:], 0.0)
 
-        n2_list = load_list(n2, "n2_list")
-        n1_list = load_list(n1, "n1_list")
-        n3_list = load_list(n3, "n3_list")
-        n4_list = load_list(n4, "n4_list")
-        n5_list = load_list(n5, "n5_list")
+        warm = sb.tile([P, 1], F32, name="warm")
+        nc.scalar.activation(warm[:], a_rows[0][:, S : S + 1], ACT.Tanh)
 
         w_bf = sb.tile([P, PLANES * N], BF16, name="w_bf", align_bytes=64)
         nc.scalar.copy(
@@ -83,23 +84,33 @@ def tile_picked_twpqsoftbdot_none_p_kernel(tc, x_words, x_scales, d_words, d_sca
         nc.vector.tensor_copy(d_scale_picked[:, H:], d_scale_table[:].indirect(k1_list[:]))
         d_scale_dealt = sb.tile([P, 2 * H], U8, name="d_scale_dealt", align_bytes=64)
         nc.vector.tensor_copy(
-            d_scale_dealt[:].rearrange("p (t mm i) -> p mm t i", t=PLANES, i=16),
-            d_scale_picked[:].rearrange("p (mm i t) -> p mm t i", t=PLANES, i=16),
+            d_scale_dealt[:].bitcast(I32).rearrange("p (t q e) -> p q t e", t=PLANES, e=2),
+            d_scale_picked[:].bitcast(I32).rearrange("p (q t e) -> p q t e", t=PLANES, e=2),
         )
-        for r in range(2):
-            nc.sync.dma_start(d_scale_dealt[2 + r : P : 32, :].bitcast(I32), d_scale_dealt[16 + r : P : 32, :].bitcast(I32))
+        for q in range(4):
+            nc.sync.dma_start(d_scale_dealt[32 * q + 4 : 32 * q + 8, :].bitcast(I32), d_scale_dealt[32 * q : 32 * q + 32 : 8, :].bitcast(I32))
 
-        def coded_product(which, k_list, x_list, name, d_picked):
+        n2_list = load_list(n2, "n2_list")
+        n1_list = load_list(n1, "n1_list")
+        n3_list = load_list(n3, "n3_list")
+        n4_list = load_list(n4, "n4_list")
+        n5_list = load_list(n5, "n5_list")
+
+        def pick_codewords(k_list, name):
+            picked = sb.tile([P, H], U32, name=f"d_picked_{name}", align_bytes=64)
+            nc.vector.tensor_copy(picked[:], d_word_table[:].indirect(k_list[:]))
+            dealt = sb.tile([P, H], U32, name=f"d_dealt_{name}", align_bytes=64)
+            nc.vector.tensor_copy(
+                dealt[:].rearrange("p (t q e) -> p q t e", t=PLANES, e=8),
+                picked[:].rearrange("p (q t e) -> p q t e", t=PLANES, e=8),
+            )
+            return dealt
+
+        def coded_product(which, d_dealt, x_list, name):
             x_picked = sb.tile([P, S], U32, name=f"x_picked_{name}", align_bytes=64)
             nc.vector.tensor_copy(x_picked[:], x_word_table[:].indirect(x_list[:]))
             x_scale_picked = sb.tile([P, S], U8, name=f"x_scale_picked_{name}", align_bytes=64)
             nc.vector.tensor_copy(x_scale_picked[:], x_scale_table[:].indirect(x_list[:]))
-            nc.vector.tensor_copy(d_picked[:], d_word_table[:].indirect(k_list[:]))
-            d_dealt = sb.tile([P, H], U32, name=f"d_dealt_{name}", align_bytes=64)
-            nc.vector.tensor_copy(
-                d_dealt[:].rearrange("p (t mm i) -> p mm t i", t=PLANES, i=4),
-                d_picked[:].rearrange("p (mm i t) -> p mm t i", t=PLANES, i=4),
-            )
             banks = []
             for t in range(PLANES):
                 bank = psum.tile([P, S], F32, name=f"bank_{name}{t}", tag=f"bank_{name}{t}")
@@ -107,7 +118,7 @@ def tile_picked_twpqsoftbdot_none_p_kernel(tc, x_words, x_scales, d_words, d_sca
                 nc.tensor.matmul_mx(
                     out=bank[:],
                     lhsT=d_dealt[:, t * P : (t + 1) * P].bitcast(FP8X4),
-                    lhsT_scale=d_scale_dealt[:, first : first + P],
+                    lhsT_scale=d_scale_dealt[4:, first : first + P],
                     rhs=x_picked[:].bitcast(FP8X4),
                     rhs_scale=x_scale_picked[:],
                     start=True,
@@ -116,49 +127,46 @@ def tile_picked_twpqsoftbdot_none_p_kernel(tc, x_words, x_scales, d_words, d_sca
                 banks.append(bank)
             return banks
 
-        b_banks = coded_product(0, k2_list, two_list, "b", sb.tile([P, H], U32, name="d_picked_b", align_bytes=64))
+        d_for_b = pick_codewords(k2_list, "b")
+        d_for_a = pick_codewords(k1_list, "a")
+        b_banks = coded_product(0, d_for_b, two_list, "b")
+        a_banks = coded_product(1, d_for_a, offs_list, "a")
+
         tanh_b = sb.tile([P, PLANES, S], F32, name="tanh_b", align_bytes=64)
-        b_rows = [sb.tile([P, S], F32, name=f"b_rows{t}", align_bytes=64) for t in range(PLANES)]
         for t in range(PLANES):
             nc.scalar.activation(tanh_b[:, t, :], b_banks[t][:], ACT.Tanh, scale=0.0625)
-            nc.scalar.activation(b_rows[t][:], b_banks[t][:], ACT.Copy, scale=gain16[:, t : t + 1])
-        b_picked = sb.tile([P, SCALAR_N2_PLANES, S], F32, name="b_picked", align_bytes=64)
-        for t in range(SCALAR_N2_PLANES):
-            for half in range(2):
-                cols = slice(half * HALF, (half + 1) * HALF)
-                nc.scalar.activation(b_picked[:, t, cols], b_rows[t][:].indirect(half_of(n2_list, half)), ACT.Copy)
-
-        a_banks = coded_product(1, k1_list, offs_list, "a", reused.tile([P, H], U32, name="d_picked_a", align_bytes=64, offset=0))
+            nc.scalar.activation(b_rows[t][:, :S], b_banks[t][:], ACT.Copy, scale=gain16[:, t : t + 1])
 
         w_codes = reused.tile([P, N], U32, name="w_codes", align_bytes=64, offset=0)
         w_scales = sb.tile([P, N], U8, name="w_scales", align_bytes=64)
         nc.vector.quantize_mx(out=w_codes[:].bitcast(FP8X4), scales=w_scales[:], in_=w_bf[:])
 
-        a_rows = [sb.tile([P, S], F32, name=f"a_rows{t}", align_bytes=64) for t in range(PLANES)]
-        for t in range(PLANES):
-            nc.vector.tensor_scalar(a_rows[t][:], a_banks[t][:], gain16[:, t : t + 1], None, ALU.mult)
-
-        gated = sb.tile([P, PLANES, S], F32, name="gated", align_bytes=64)
-        nc.vector.tensor_tensor(gated[:, :SCALAR_N2_PLANES, :], b_picked[:], tanh_b[:, :SCALAR_N2_PLANES, :], ALU.mult)
-
         a_picked = sb.tile([P, PLANES, S], F32, name="a_picked", align_bytes=64)
+        gated = sb.tile([P, PLANES, S], F32, name="gated", align_bytes=64)
+        for t in range(PLANES):
+            if t < VECTOR_A_COPIES:
+                nc.vector.tensor_scalar(a_rows[t][:, :S], a_banks[t][:], gain16[:, t : t + 1], None, ALU.mult)
+            else:
+                nc.scalar.activation(a_rows[t][:, :S], a_banks[t][:], ACT.Copy, scale=gain16[:, t : t + 1])
+        for t in range(PLANES):
+            nc.scalar.activation(a_picked[:, t, :], a_rows[t][:].indirect(n1_list[:]), ACT.Copy)
+            nc.vector.tensor_tensor(gated[:, t, :], b_rows[t][:].indirect(n2_list[:]), tanh_b[:, t, :], ALU.mult)
+
         h_banks = [psum.tile([P, S], F32, name=f"bank_h{t}", tag=f"bank_b{t}") for t in range(PLANES)]
+        z_bf = [sb.tile([P, HALF * PLANES], BF16, name=f"z_bf{half}", align_bytes=64) for half in range(2)]
         for half in range(2):
             cols = slice(half * HALF, (half + 1) * HALF)
-            for t in range(PLANES):
-                nc.scalar.activation(a_picked[:, t, cols], a_rows[t][:].indirect(half_of(n1_list, half)), ACT.Copy)
-            for t in range(SCALAR_N2_PLANES, PLANES):
-                nc.vector.tensor_tensor(gated[:, t, cols], b_rows[t][:].indirect(half_of(n2_list, half)), tanh_b[:, t, cols], ALU.mult)
-            z_bf = sb.tile([P, HALF * PLANES], BF16, name=f"z_bf{half}", align_bytes=64)
             nc.vector.tensor_tensor(
-                z_bf[:].rearrange("p (c i t) -> p c t i", t=PLANES, i=4),
+                z_bf[half][:].rearrange("p (c i t) -> p c t i", t=PLANES, i=4),
                 a_picked[:, :, cols].rearrange("p t (c i) -> p c t i", i=4),
                 gated[:, :, cols].rearrange("p t (c i) -> p c t i", i=4),
                 ALU.subtract,
             )
+        for half in range(2):
+            cols = slice(half * HALF, (half + 1) * HALF)
             z_codes = sb.tile([P, HALF], U32, name=f"z_codes{half}", align_bytes=64)
             z_scales = sb.tile([P, HALF], U8, name=f"z_scales{half}", align_bytes=64)
-            nc.vector.quantize_mx(out=z_codes[:].bitcast(FP8X4), scales=z_scales[:], in_=z_bf[:])
+            nc.vector.quantize_mx(out=z_codes[:].bitcast(FP8X4), scales=z_scales[:], in_=z_bf[half][:])
             for t in range(PLANES):
                 nc.tensor.matmul_mx(
                     out=h_banks[t][:, cols],
@@ -175,14 +183,20 @@ def tile_picked_twpqsoftbdot_none_p_kernel(tc, x_words, x_scales, d_words, d_sca
             nc.vector.tensor_copy(h_rows[t][:, :S], h_banks[t][:])
         for t in range(PLANES):
             picked = []
-            for name, offsets in (("n3", n3_list), ("n4", n4_list), ("n5", n5_list)):
+            for name, offsets in (("n3", n3_list), ("n4", n4_list)):
                 tile = sb.tile([P, S], F32, name=f"h_{name}_{t}", align_bytes=64)
                 nc.scalar.activation(tile[:], h_rows[t][:].indirect(offsets[:]), ACT.Copy)
                 picked.append(tile)
             first = sb.tile([P, S], F32, name=f"first{t}", align_bytes=64)
             nc.vector.scalar_tensor_tensor(first[:], picked[0][:], 0.75, h_rows[t][:, :S], ALU.mult, ALU.mult)
-            second = sb.tile([P, S], F32, name=f"second{t}", align_bytes=64)
-            nc.vector.scalar_tensor_tensor(second[:], picked[1][:], 0.75, picked[2][:], ALU.mult, ALU.mult)
-            result = sb.tile([P, S], F32, name=f"result{t}", align_bytes=64)
-            nc.vector.tensor_tensor(result[:], first[:], second[:], ALU.add)
-            nc.sync.dma_start(out_rows[t], result[:])
+            pieces = 2 if t == PLANES - 1 else 1
+            width = S // pieces
+            for piece in range(pieces):
+                cols = slice(piece * width, (piece + 1) * width)
+                h_n5 = sb.tile([P, width], F32, name=f"h_n5_{t}_{piece}", align_bytes=64)
+                nc.scalar.activation(h_n5[:], h_rows[t][:].indirect(n5_list[:, piece * width // 16 : (piece + 1) * width // 16]), ACT.Copy)
+                second = sb.tile([P, width], F32, name=f"second{t}_{piece}", align_bytes=64)
+                nc.vector.scalar_tensor_tensor(second[:], picked[1][:, cols], 0.75, h_n5[:], ALU.mult, ALU.mult)
+                result = sb.tile([P, width], F32, name=f"result{t}_{piece}", align_bytes=64)
+                nc.vector.tensor_tensor(result[:], first[:, cols], second[:], ALU.add)
+                nc.sync.dma_start(out_rows[t][:, cols], result[:])

@@ -1,7 +1,6 @@
 from contextlib import ExitStack
 
 import concourse.mybir as mybir
-from concourse.masks import make_identity
 
 K, T, S, N, G, H = 512, 1024, 256, 512, 2048, 512
 FLOPS = 2 * K * H * S * 2 + 2 * H * N * S
@@ -29,6 +28,7 @@ def tile_picked_twpqsoftbdot_none_p_kernel(tc, x_words, x_scales, d_words, d_sca
         lists = ctx.enter_context(tc.tile_pool(name="lists", bufs=1))
         sb = ctx.enter_context(tc.tile_pool(name="sb", bufs=1))
         reused = ctx.enter_context(tc.tile_pool(name="reused", bufs=1))
+        reused_w = ctx.enter_context(tc.tile_pool(name="reused_w", bufs=1))
         psum = ctx.enter_context(tc.psum_pool(name="psum", bufs=1))
 
         def load_list(src, name):
@@ -40,29 +40,21 @@ def tile_picked_twpqsoftbdot_none_p_kernel(tc, x_words, x_scales, d_words, d_sca
         d_scale_table = sb.tile([P, G], U8, name="d_scale_table", align_bytes=64)
         nc.sync.dma_start(d_scale_table[:].bitcast(I32), d_scales[0].bitcast(I32).unsqueeze(1).to_broadcast([16, 8, G // 4]))
         k1_list = load_list(k1, "k1_list")
-        d_word_table = sb.tile([P, G], U32, name="d_word_table", align_bytes=64)
-        nc.sync.dma_start(d_word_table[:].bitcast(I32), d_words[0].rearrange("p n t -> p (n t)").bitcast(I32))
-        w_raw = sb.tile([P, PLANES, N], F32, name="w_raw", align_bytes=64)
-        for j in range(PLANES):
-            nc.sync.dma_start(w_raw[:, j, :], w1.rearrange("(q j e) m -> j q e m", j=PLANES, e=8)[j])
-        x_word_table = reused.tile([P, T], U32, name="x_word_table", align_bytes=64, offset=T)
-        nc.sync.dma_start(x_word_table[:].bitcast(I32), x_words[0].rearrange("p n t -> p (n t)").bitcast(I32))
         two_list = load_list(two, "two_list")
-        offs_list = load_list(offs, "offs_list")
-
-        gain_rows = sb.tile([P, P], F32, name="gain_rows", align_bytes=64)
-        nc.gpsimd.memset(gain_rows[:], 0.0)
-        nc.gpsimd.dma_start(gain_rows[:PLANES, :].rearrange("t (q e) -> t q e", e=8), gn.rearrange("(q t e) o -> t q (e o)", t=PLANES, e=8))
+        w_raw = reused_w.tile([P, PLANES, N], F32, name="w_raw", align_bytes=64, offset=0)
+        nc.sync.dma_start(w_raw[:], w1.rearrange("(p j) m -> p j m", j=PLANES))
         x_scale_table = reused.tile([P, T], U8, name="x_scale_table", align_bytes=64, offset=0)
         for q in range(4):
             rows = x_scales[0].bitcast(I32)[4 * q : 4 * q + 4, :]
-            nc.gpsimd.dma_start(x_scale_table[32 * q : 32 * q + 32, :].bitcast(I32), rows.unsqueeze(0).to_broadcast([8, 4, T // 4]))
-        identity = sb.tile([P, P], F32, name="identity", align_bytes=64)
-        make_identity(nc, identity[:])
-        gain_bank = psum.tile([P, P], F32, name="gain_bank", tag="bank_a3")
-        nc.tensor.transpose(gain_bank[:], gain_rows[:], identity[:])
-        gain16 = sb.tile([P, PLANES], F32, name="gain16")
-        nc.scalar.activation(gain16[:], gain_bank[:, :PLANES], ACT.Copy, scale=0.0625)
+            nc.sync.dma_start(x_scale_table[32 * q : 32 * q + 32, :].bitcast(I32), rows.unsqueeze(0).to_broadcast([8, 4, T // 4]))
+        offs_list = load_list(offs, "offs_list")
+        d_word_table = sb.tile([P, G], U32, name="d_word_table", align_bytes=64)
+        nc.sync.dma_start(d_word_table[:].bitcast(I32), d_words[0].rearrange("p n t -> p (n t)").bitcast(I32))
+        x_word_table = reused.tile([P, T], U32, name="x_word_table", align_bytes=64, offset=T)
+        nc.sync.dma_start(x_word_table[:].bitcast(I32), x_words[0].rearrange("p n t -> p (n t)").bitcast(I32))
+        gain = sb.tile([P, PLANES], F32, name="gain", align_bytes=64)
+        nc.sync.dma_start(gain[:], gn.rearrange("(p t) o -> p (t o)", t=PLANES))
+        gain16 = reused_w.tile([P, PLANES], F32, name="gain16", align_bytes=64, offset=0)
 
         a_rows = [sb.tile([P, S + SPARE], F32, name=f"a_rows{t}", align_bytes=64) for t in range(PLANES)]
         b_rows = [sb.tile([P, S + SPARE], F32, name=f"b_rows{t}", align_bytes=64) for t in range(PLANES)]
@@ -74,18 +66,19 @@ def tile_picked_twpqsoftbdot_none_p_kernel(tc, x_words, x_scales, d_words, d_sca
         nc.scalar.activation(warm[:], a_rows[0][:, S : S + 1], ACT.Tanh)
 
         w_bf = sb.tile([P, PLANES * N], BF16, name="w_bf", align_bytes=64)
-        nc.scalar.copy(
-            w_bf[:].rearrange("p (t m j) -> p m j t", t=PLANES, j=PLANES),
-            w_raw[:].rearrange("p j (m t) -> p m j t", t=PLANES),
-        )
+        w_out = w_bf[:].rearrange("p (t u e i j) -> p t u e j i", t=PLANES, e=2, i=4, j=PLANES)
+        w_in = w_raw[:].rearrange("p j (u t e i) -> p t u e j i", t=PLANES, e=2, i=4)
+        for t in range(PLANES):
+            nc.scalar.copy(w_out[:, t], w_in[:, t])
+        nc.scalar.activation(gain16[:], gain[:], ACT.Copy, scale=0.0625)
 
         d_scale_picked = sb.tile([P, 2 * H], U8, name="d_scale_picked", align_bytes=64)
         nc.vector.tensor_copy(d_scale_picked[:, :H], d_scale_table[:].indirect(k2_list[:]))
         nc.vector.tensor_copy(d_scale_picked[:, H:], d_scale_table[:].indirect(k1_list[:]))
         d_scale_dealt = sb.tile([P, 2 * H], U8, name="d_scale_dealt", align_bytes=64)
         nc.vector.tensor_copy(
-            d_scale_dealt[:].bitcast(I32).rearrange("p (t q e) -> p q t e", t=PLANES, e=2),
-            d_scale_picked[:].bitcast(I32).rearrange("p (q t e) -> p q t e", t=PLANES, e=2),
+            d_scale_dealt[:].rearrange("p (t mm i) -> p mm t i", t=PLANES, i=16),
+            d_scale_picked[:].rearrange("p (mm i t) -> p mm t i", t=PLANES, i=16),
         )
         for q in range(4):
             nc.sync.dma_start(d_scale_dealt[32 * q + 4 : 32 * q + 8, :].bitcast(I32), d_scale_dealt[32 * q : 32 * q + 32 : 8, :].bitcast(I32))
@@ -96,21 +89,23 @@ def tile_picked_twpqsoftbdot_none_p_kernel(tc, x_words, x_scales, d_words, d_sca
         n4_list = load_list(n4, "n4_list")
         n5_list = load_list(n5, "n5_list")
 
-        def pick_codewords(k_list, name):
-            picked = sb.tile([P, H], U32, name=f"d_picked_{name}", align_bytes=64)
+        def pick_codewords(k_list, name, picked):
             nc.vector.tensor_copy(picked[:], d_word_table[:].indirect(k_list[:]))
             dealt = sb.tile([P, H], U32, name=f"d_dealt_{name}", align_bytes=64)
             nc.vector.tensor_copy(
-                dealt[:].rearrange("p (t q e) -> p q t e", t=PLANES, e=8),
-                picked[:].rearrange("p (q t e) -> p q t e", t=PLANES, e=8),
+                dealt[:].rearrange("p (t mm i) -> p mm t i", t=PLANES, i=4),
+                picked[:].rearrange("p (mm i t) -> p mm t i", t=PLANES, i=4),
             )
             return dealt
 
-        def coded_product(which, d_dealt, x_list, name):
+        def pick_tokens(x_list, name):
             x_picked = sb.tile([P, S], U32, name=f"x_picked_{name}", align_bytes=64)
             nc.vector.tensor_copy(x_picked[:], x_word_table[:].indirect(x_list[:]))
             x_scale_picked = sb.tile([P, S], U8, name=f"x_scale_picked_{name}", align_bytes=64)
             nc.vector.tensor_copy(x_scale_picked[:], x_scale_table[:].indirect(x_list[:]))
+            return x_picked, x_scale_picked
+
+        def coded_product(which, d_dealt, x_picked, x_scale_picked, name):
             banks = []
             for t in range(PLANES):
                 bank = psum.tile([P, S], F32, name=f"bank_{name}{t}", tag=f"bank_{name}{t}")
@@ -127,10 +122,11 @@ def tile_picked_twpqsoftbdot_none_p_kernel(tc, x_words, x_scales, d_words, d_sca
                 banks.append(bank)
             return banks
 
-        d_for_b = pick_codewords(k2_list, "b")
-        d_for_a = pick_codewords(k1_list, "a")
-        b_banks = coded_product(0, d_for_b, two_list, "b")
-        a_banks = coded_product(1, d_for_a, offs_list, "a")
+        d_for_b = pick_codewords(k2_list, "b", sb.tile([P, H], U32, name="d_picked_b", align_bytes=64))
+        b_banks = coded_product(0, d_for_b, *pick_tokens(two_list, "b"), "b")
+        x_for_a = pick_tokens(offs_list, "a")
+        d_for_a = pick_codewords(k1_list, "a", reused.tile([P, H], U32, name="d_picked_a", align_bytes=64, offset=0))
+        a_banks = coded_product(1, d_for_a, *x_for_a, "a")
 
         tanh_b = sb.tile([P, PLANES, S], F32, name="tanh_b", align_bytes=64)
         for t in range(PLANES):
@@ -144,7 +140,7 @@ def tile_picked_twpqsoftbdot_none_p_kernel(tc, x_words, x_scales, d_words, d_sca
         a_picked = sb.tile([P, PLANES, S], F32, name="a_picked", align_bytes=64)
         gated = sb.tile([P, PLANES, S], F32, name="gated", align_bytes=64)
         for t in range(PLANES):
-            if t < VECTOR_A_COPIES:
+            if t >= PLANES - VECTOR_A_COPIES:
                 nc.vector.tensor_scalar(a_rows[t][:, :S], a_banks[t][:], gain16[:, t : t + 1], None, ALU.mult)
             else:
                 nc.scalar.activation(a_rows[t][:, :S], a_banks[t][:], ACT.Copy, scale=gain16[:, t : t + 1])
@@ -178,7 +174,7 @@ def tile_picked_twpqsoftbdot_none_p_kernel(tc, x_words, x_scales, d_words, d_sca
                     stop=True,
                 )
 
-        out_rows = out.rearrange("(p t) c -> t p c", t=PLANES)
+        out_rows = out.rearrange("(u t e) c -> t u e c", t=PLANES, e=8)
         for t in range(PLANES):
             nc.vector.tensor_copy(h_rows[t][:, :S], h_banks[t][:])
         for t in range(PLANES):
@@ -199,4 +195,4 @@ def tile_picked_twpqsoftbdot_none_p_kernel(tc, x_words, x_scales, d_words, d_sca
                 nc.vector.scalar_tensor_tensor(second[:], picked[1][:, cols], 0.75, h_n5[:], ALU.mult, ALU.mult)
                 result = sb.tile([P, width], F32, name=f"result{t}_{piece}", align_bytes=64)
                 nc.vector.tensor_tensor(result[:], first[:, cols], second[:], ALU.add)
-                nc.sync.dma_start(out_rows[t][:, cols], result[:])
+                nc.sync.dma_start(out_rows[t][:, :, cols], result[:])

@@ -19,7 +19,6 @@ P = 128
 PLANES = 4
 HALF = S // 2
 SPARE = 16
-VECTOR_A_COPIES = 2
 
 
 def tile_picked_twpqsoftbdot_none_p_kernel(tc, x_words, x_scales, d_words, d_scales, gn, w1, offs, k1, two, k2, n1, n2, n3, n4, n5, out):
@@ -36,22 +35,23 @@ def tile_picked_twpqsoftbdot_none_p_kernel(tc, x_words, x_scales, d_words, d_sca
             nc.sync.dma_start(tile[:], src)
             return tile
 
-        k2_list = load_list(k2, "k2_list")
         d_scale_table = sb.tile([P, G], U8, name="d_scale_table", align_bytes=64)
-        nc.sync.dma_start(d_scale_table[:].bitcast(I32), d_scales[0].bitcast(I32).unsqueeze(1).to_broadcast([16, 8, G // 4]))
+        nc.vector.memset(d_scale_table[:].bitcast(I32), 0)
+        k2_list = load_list(k2, "k2_list")
+        nc.sync.dma_start(d_scale_table[0:P:8, :].bitcast(I32), d_scales[0].bitcast(I32))
         k1_list = load_list(k1, "k1_list")
+        d_word_table = sb.tile([P, G], U32, name="d_word_table", align_bytes=64)
+        nc.sync.dma_start(d_word_table[:].bitcast(I32), d_words[0].rearrange("p n t -> p (n t)").bitcast(I32))
         two_list = load_list(two, "two_list")
         w_raw = reused_w.tile([P, PLANES, N], F32, name="w_raw", align_bytes=64, offset=0)
         nc.sync.dma_start(w_raw[:], w1.rearrange("(p j) m -> p j m", j=PLANES))
         x_scale_table = reused.tile([P, T], U8, name="x_scale_table", align_bytes=64, offset=0)
+        nc.vector.memset(x_scale_table[:].bitcast(I32), 0)
         for q in range(4):
-            rows = x_scales[0].bitcast(I32)[4 * q : 4 * q + 4, :]
-            nc.sync.dma_start(x_scale_table[32 * q : 32 * q + 32, :].bitcast(I32), rows.unsqueeze(0).to_broadcast([8, 4, T // 4]))
-        offs_list = load_list(offs, "offs_list")
-        d_word_table = sb.tile([P, G], U32, name="d_word_table", align_bytes=64)
-        nc.sync.dma_start(d_word_table[:].bitcast(I32), d_words[0].rearrange("p n t -> p (n t)").bitcast(I32))
+            nc.sync.dma_start(x_scale_table[32 * q : 32 * q + 4, :].bitcast(I32), x_scales[0].bitcast(I32)[4 * q : 4 * q + 4, :])
         x_word_table = reused.tile([P, T], U32, name="x_word_table", align_bytes=64, offset=T)
         nc.sync.dma_start(x_word_table[:].bitcast(I32), x_words[0].rearrange("p n t -> p (n t)").bitcast(I32))
+        offs_list = load_list(offs, "offs_list")
         gain = sb.tile([P, PLANES], F32, name="gain", align_bytes=64)
         nc.sync.dma_start(gain[:], gn.rearrange("(p t) o -> p (t o)", t=PLANES))
         gain16 = reused_w.tile([P, PLANES], F32, name="gain16", align_bytes=64, offset=0)
@@ -89,7 +89,8 @@ def tile_picked_twpqsoftbdot_none_p_kernel(tc, x_words, x_scales, d_words, d_sca
         n4_list = load_list(n4, "n4_list")
         n5_list = load_list(n5, "n5_list")
 
-        def pick_codewords(k_list, name, picked):
+        def pick_codewords(k_list, name):
+            picked = sb.tile([P, H], U32, name=f"d_picked_{name}", align_bytes=64)
             nc.vector.tensor_copy(picked[:], d_word_table[:].indirect(k_list[:]))
             dealt = sb.tile([P, H], U32, name=f"d_dealt_{name}", align_bytes=64)
             nc.vector.tensor_copy(
@@ -122,11 +123,10 @@ def tile_picked_twpqsoftbdot_none_p_kernel(tc, x_words, x_scales, d_words, d_sca
                 banks.append(bank)
             return banks
 
-        d_for_b = pick_codewords(k2_list, "b", sb.tile([P, H], U32, name="d_picked_b", align_bytes=64))
+        d_for_b = pick_codewords(k2_list, "b")
+        d_for_a = pick_codewords(k1_list, "a")
         b_banks = coded_product(0, d_for_b, *pick_tokens(two_list, "b"), "b")
-        x_for_a = pick_tokens(offs_list, "a")
-        d_for_a = pick_codewords(k1_list, "a", reused.tile([P, H], U32, name="d_picked_a", align_bytes=64, offset=0))
-        a_banks = coded_product(1, d_for_a, *x_for_a, "a")
+        a_banks = coded_product(1, d_for_a, *pick_tokens(offs_list, "a"), "a")
 
         tanh_b = sb.tile([P, PLANES, S], F32, name="tanh_b", align_bytes=64)
         for t in range(PLANES):
@@ -140,7 +140,7 @@ def tile_picked_twpqsoftbdot_none_p_kernel(tc, x_words, x_scales, d_words, d_sca
         a_picked = sb.tile([P, PLANES, S], F32, name="a_picked", align_bytes=64)
         gated = sb.tile([P, PLANES, S], F32, name="gated", align_bytes=64)
         for t in range(PLANES):
-            if t >= PLANES - VECTOR_A_COPIES:
+            if t < PLANES - 1:
                 nc.vector.tensor_scalar(a_rows[t][:, :S], a_banks[t][:], gain16[:, t : t + 1], None, ALU.mult)
             else:
                 nc.scalar.activation(a_rows[t][:, :S], a_banks[t][:], ACT.Copy, scale=gain16[:, t : t + 1])
@@ -173,9 +173,10 @@ def tile_picked_twpqsoftbdot_none_p_kernel(tc, x_words, x_scales, d_words, d_sca
                     start=True,
                     stop=True,
                 )
+            nc.scalar.copy(h_rows[0][:, cols], h_banks[0][:, cols])
 
         out_rows = out.rearrange("(u t e) c -> t u e c", t=PLANES, e=8)
-        for t in range(PLANES):
+        for t in range(1, PLANES):
             nc.vector.tensor_copy(h_rows[t][:, :S], h_banks[t][:])
         for t in range(PLANES):
             picked = []

from contextlib import ExitStack

import concourse.mybir as mybir

K, T, S, N, G, H = 512, 1024, 256, 512, 2048, 512
FLOPS = 2 * K * H * S * 2 + 2 * H * N * S

F32 = mybir.dt.float32
BF16 = mybir.dt.bfloat16
I32 = mybir.dt.int32
U32 = mybir.dt.uint32
U16 = mybir.dt.uint16
U8 = mybir.dt.uint8
FP8X4 = mybir.dt.float8_e4m3fn_x4
ALU = mybir.AluOpType
ACT = mybir.ActivationFunctionType

P = 128
PLANES = 4
HALF = S // 2
SPARE = 16


def tile_picked_twpqsoftbdot_none_p_kernel(tc, x_words, x_scales, d_words, d_scales, gn, w1, offs, k1, two, k2, n1, n2, n3, n4, n5, out):
    nc = tc.nc
    with ExitStack() as ctx:
        lists = ctx.enter_context(tc.tile_pool(name="lists", bufs=1))
        sb = ctx.enter_context(tc.tile_pool(name="sb", bufs=1))
        reused = ctx.enter_context(tc.tile_pool(name="reused", bufs=1))
        reused_w = ctx.enter_context(tc.tile_pool(name="reused_w", bufs=1))
        psum = ctx.enter_context(tc.psum_pool(name="psum", bufs=1))

        def load_list(src, name):
            tile = lists.tile(list(src.shape), U16, name=name)
            nc.sync.dma_start(tile[:], src)
            return tile

        d_scale_table = sb.tile([P, G], U8, name="d_scale_table", align_bytes=64)
        nc.vector.memset(d_scale_table[:].bitcast(I32), 0)
        k2_list = load_list(k2, "k2_list")
        nc.sync.dma_start(d_scale_table[0:P:8, :].bitcast(I32), d_scales[0].bitcast(I32))
        k1_list = load_list(k1, "k1_list")
        d_word_table = sb.tile([P, G], U32, name="d_word_table", align_bytes=64)
        nc.sync.dma_start(d_word_table[:].bitcast(I32), d_words[0].rearrange("p n t -> p (n t)").bitcast(I32))
        two_list = load_list(two, "two_list")
        w_raw = reused_w.tile([P, PLANES, N], F32, name="w_raw", align_bytes=64, offset=0)
        nc.sync.dma_start(w_raw[:], w1.rearrange("(p j) m -> p j m", j=PLANES))
        x_scale_table = reused.tile([P, T], U8, name="x_scale_table", align_bytes=64, offset=0)
        nc.vector.memset(x_scale_table[:].bitcast(I32), 0)
        for q in range(4):
            nc.sync.dma_start(x_scale_table[32 * q : 32 * q + 4, :].bitcast(I32), x_scales[0].bitcast(I32)[4 * q : 4 * q + 4, :])
        x_word_table = reused.tile([P, T], U32, name="x_word_table", align_bytes=64, offset=T)
        nc.sync.dma_start(x_word_table[:].bitcast(I32), x_words[0].rearrange("p n t -> p (n t)").bitcast(I32))
        offs_list = load_list(offs, "offs_list")
        gain = sb.tile([P, PLANES], F32, name="gain", align_bytes=64)
        nc.sync.dma_start(gain[:], gn.rearrange("(p t) o -> p (t o)", t=PLANES))
        gain16 = reused_w.tile([P, PLANES], F32, name="gain16", align_bytes=64, offset=0)

        a_rows = [sb.tile([P, S + SPARE], F32, name=f"a_rows{t}", align_bytes=64) for t in range(PLANES)]
        b_rows = [sb.tile([P, S + SPARE], F32, name=f"b_rows{t}", align_bytes=64) for t in range(PLANES)]
        h_rows = [sb.tile([P, 2 * S], F32, name=f"h_rows{t}", align_bytes=64) for t in range(PLANES)]
        for window in a_rows + b_rows + h_rows:
            nc.vector.memset(window[:, S:], 0.0)

        warm = sb.tile([P, 1], F32, name="warm")
        nc.scalar.activation(warm[:], a_rows[0][:, S : S + 1], ACT.Tanh)

        w_bf = sb.tile([P, PLANES * N], BF16, name="w_bf", align_bytes=64)
        w_out = w_bf[:].rearrange("p (t u e i j) -> p t u e j i", t=PLANES, e=2, i=4, j=PLANES)
        w_in = w_raw[:].rearrange("p j (u t e i) -> p t u e j i", t=PLANES, e=2, i=4)
        for t in range(PLANES):
            nc.scalar.copy(w_out[:, t], w_in[:, t])
        nc.scalar.activation(gain16[:], gain[:], ACT.Copy, scale=0.0625)

        d_scale_picked = sb.tile([P, 2 * H], U8, name="d_scale_picked", align_bytes=64)
        nc.vector.tensor_copy(d_scale_picked[:, :H], d_scale_table[:].indirect(k2_list[:]))
        nc.vector.tensor_copy(d_scale_picked[:, H:], d_scale_table[:].indirect(k1_list[:]))
        d_scale_dealt = sb.tile([P, 2 * H], U8, name="d_scale_dealt", align_bytes=64)
        nc.vector.tensor_copy(
            d_scale_dealt[:].rearrange("p (t mm i) -> p mm t i", t=PLANES, i=16),
            d_scale_picked[:].rearrange("p (mm i t) -> p mm t i", t=PLANES, i=16),
        )
        for q in range(4):
            nc.sync.dma_start(d_scale_dealt[32 * q + 4 : 32 * q + 8, :].bitcast(I32), d_scale_dealt[32 * q : 32 * q + 32 : 8, :].bitcast(I32))

        n2_list = load_list(n2, "n2_list")
        n1_list = load_list(n1, "n1_list")
        n3_list = load_list(n3, "n3_list")
        n4_list = load_list(n4, "n4_list")
        n5_list = load_list(n5, "n5_list")

        def pick_codewords(k_list, name):
            picked = sb.tile([P, H], U32, name=f"d_picked_{name}", align_bytes=64)
            nc.vector.tensor_copy(picked[:], d_word_table[:].indirect(k_list[:]))
            dealt = sb.tile([P, H], U32, name=f"d_dealt_{name}", align_bytes=64)
            nc.vector.tensor_copy(
                dealt[:].rearrange("p (t mm i) -> p mm t i", t=PLANES, i=4),
                picked[:].rearrange("p (mm i t) -> p mm t i", t=PLANES, i=4),
            )
            return dealt

        def pick_tokens(x_list, name):
            x_picked = sb.tile([P, S], U32, name=f"x_picked_{name}", align_bytes=64)
            nc.vector.tensor_copy(x_picked[:], x_word_table[:].indirect(x_list[:]))
            x_scale_picked = sb.tile([P, S], U8, name=f"x_scale_picked_{name}", align_bytes=64)
            nc.vector.tensor_copy(x_scale_picked[:], x_scale_table[:].indirect(x_list[:]))
            return x_picked, x_scale_picked

        def coded_product(which, d_dealt, x_picked, x_scale_picked, name):
            banks = []
            for t in range(PLANES):
                bank = psum.tile([P, S], F32, name=f"bank_{name}{t}", tag=f"bank_{name}{t}")
                first = (2 * t + which) * P
                nc.tensor.matmul_mx(
                    out=bank[:],
                    lhsT=d_dealt[:, t * P : (t + 1) * P].bitcast(FP8X4),
                    lhsT_scale=d_scale_dealt[4:, first : first + P],
                    rhs=x_picked[:].bitcast(FP8X4),
                    rhs_scale=x_scale_picked[:],
                    start=True,
                    stop=True,
                )
                banks.append(bank)
            return banks

        d_for_b = pick_codewords(k2_list, "b")
        d_for_a = pick_codewords(k1_list, "a")
        b_banks = coded_product(0, d_for_b, *pick_tokens(two_list, "b"), "b")
        a_banks = coded_product(1, d_for_a, *pick_tokens(offs_list, "a"), "a")

        tanh_b = sb.tile([P, PLANES, S], F32, name="tanh_b", align_bytes=64)
        for t in range(PLANES):
            nc.scalar.activation(tanh_b[:, t, :], b_banks[t][:], ACT.Tanh, scale=0.0625)
            nc.scalar.activation(b_rows[t][:, :S], b_banks[t][:], ACT.Copy, scale=gain16[:, t : t + 1])

        w_codes = reused.tile([P, N], U32, name="w_codes", align_bytes=64, offset=0)
        w_scales = sb.tile([P, N], U8, name="w_scales", align_bytes=64)
        nc.vector.quantize_mx(out=w_codes[:].bitcast(FP8X4), scales=w_scales[:], in_=w_bf[:])

        a_picked = sb.tile([P, PLANES, S], F32, name="a_picked", align_bytes=64)
        gated = sb.tile([P, PLANES, S], F32, name="gated", align_bytes=64)
        for t in range(PLANES):
            if t < PLANES - 1:
                nc.vector.tensor_scalar(a_rows[t][:, :S], a_banks[t][:], gain16[:, t : t + 1], None, ALU.mult)
            else:
                nc.scalar.activation(a_rows[t][:, :S], a_banks[t][:], ACT.Copy, scale=gain16[:, t : t + 1])
        for t in range(PLANES):
            nc.scalar.activation(a_picked[:, t, :], a_rows[t][:].indirect(n1_list[:]), ACT.Copy)
            nc.vector.tensor_tensor(gated[:, t, :], b_rows[t][:].indirect(n2_list[:]), tanh_b[:, t, :], ALU.mult)

        h_banks = [psum.tile([P, S], F32, name=f"bank_h{t}", tag=f"bank_b{t}") for t in range(PLANES)]
        z_bf = [sb.tile([P, HALF * PLANES], BF16, name=f"z_bf{half}", align_bytes=64) for half in range(2)]
        for half in range(2):
            cols = slice(half * HALF, (half + 1) * HALF)
            nc.vector.tensor_tensor(
                z_bf[half][:].rearrange("p (c i t) -> p c t i", t=PLANES, i=4),
                a_picked[:, :, cols].rearrange("p t (c i) -> p c t i", i=4),
                gated[:, :, cols].rearrange("p t (c i) -> p c t i", i=4),
                ALU.subtract,
            )
        for half in range(2):
            cols = slice(half * HALF, (half + 1) * HALF)
            z_codes = sb.tile([P, HALF], U32, name=f"z_codes{half}", align_bytes=64)
            z_scales = sb.tile([P, HALF], U8, name=f"z_scales{half}", align_bytes=64)
            nc.vector.quantize_mx(out=z_codes[:].bitcast(FP8X4), scales=z_scales[:], in_=z_bf[half][:])
            for t in range(PLANES):
                nc.tensor.matmul_mx(
                    out=h_banks[t][:, cols],
                    lhsT=w_codes[:, t * P : (t + 1) * P].bitcast(FP8X4),
                    lhsT_scale=w_scales[:, t * P : (t + 1) * P],
                    rhs=z_codes[:].bitcast(FP8X4),
                    rhs_scale=z_scales[:],
                    start=True,
                    stop=True,
                )
            nc.scalar.copy(h_rows[0][:, cols], h_banks[0][:, cols])

        out_rows = out.rearrange("(u t e) c -> t u e c", t=PLANES, e=8)
        for t in range(1, PLANES):
            nc.vector.tensor_copy(h_rows[t][:, :S], h_banks[t][:])
        for t in range(PLANES):
            picked = []
            for name, offsets in (("n3", n3_list), ("n4", n4_list)):
                tile = sb.tile([P, S], F32, name=f"h_{name}_{t}", align_bytes=64)
                nc.scalar.activation(tile[:], h_rows[t][:].indirect(offsets[:]), ACT.Copy)
                picked.append(tile)
            first = sb.tile([P, S], F32, name=f"first{t}", align_bytes=64)
            nc.vector.scalar_tensor_tensor(first[:], picked[0][:], 0.75, h_rows[t][:, :S], ALU.mult, ALU.mult)
            pieces = 2 if t == PLANES - 1 else 1
            width = S // pieces
            for piece in range(pieces):
                cols = slice(piece * width, (piece + 1) * width)
                h_n5 = sb.tile([P, width], F32, name=f"h_n5_{t}_{piece}", align_bytes=64)
                nc.scalar.activation(h_n5[:], h_rows[t][:].indirect(n5_list[:, piece * width // 16 : (piece + 1) * width // 16]), ACT.Copy)
                second = sb.tile([P, width], F32, name=f"second{t}_{piece}", align_bytes=64)
                nc.vector.scalar_tensor_tensor(second[:], picked[1][:, cols], 0.75, h_n5[:], ALU.mult, ALU.mult)
                result = sb.tile([P, width], F32, name=f"result{t}_{piece}", align_bytes=64)
                nc.vector.tensor_tensor(result[:], first[:, cols], second[:], ALU.add)
                nc.sync.dma_start(out_rows[t][:, :, cols], result[:])
